import numpy as np
CORES = [0,1,2,3,4,5,6,7]
N = 8
def setup_inputs(rng):
    return {"x1": rng.standard_normal((N, 128, 256), dtype=np.float32), "x2": rng.standard_normal((N, 128, 2), dtype=np.float32), "x3": rng.standard_normal((N, 128, 64), dtype=np.float32)}
def reference(x1, x2, x3):
    out = {}
    s = x1.sum(axis=0, dtype=np.float64).astype(x1.dtype)
    out["y1"] = np.broadcast_to(s, (N,) + s.shape)
    s = x2.sum(axis=0, dtype=np.float64).astype(x2.dtype)
    out["y2"] = np.broadcast_to(s, (N,) + s.shape)
    s = x3.sum(axis=0, dtype=np.float64).astype(x3.dtype)
    out["y3"] = np.broadcast_to(s, (N,) + s.shape)
    return out

@@ -1,0 +1,67 @@
+from concourse.bass import DstId, RemoteDMATransfer
+
+W = 81
+NB = 4
+C1, C3, C2 = 0, 256, 320
+
+SCRATCH = {
+    "pack": ("sbuf", [128, NB * W], "float32"),
+    "land": ("sbuf", [128, 8 * W], "float32"),
+    "res": ("sbuf", [128, NB * W], "float32"),
+}
+SEMAPHORES = ["loaded", "arrived", "summed", "sent", "stored"]
+
+
+def rank_program(g, core, T, topo):
+    if T.rank_of(core) is None:
+        return
+    sem = T.sem
+
+    def dst(c):
+        rid, pid, _se = topo.addr(c)
+        return DstId(rid=rid, pnc=pid)
+
+    def blk(buf, k):
+        return buf[:, k * W:(k + 1) * W]
+
+    mine = core % NB
+    partner = (core + NB) % 8
+
+    g.sync.dma_start(T.pack[:, C1:C1 + 256], T.x1[:, :]).then_inc(sem.loaded, 16)
+    g.scalar.dma_start(T.pack[:, C3:C3 + 64], T.x3[:, :]).then_inc(sem.loaded, 16)
+    g.scalar.dma_start(T.pack[:, C2:C2 + 2], T.x2[:, :]).then_inc(sem.loaded, 16)
+    g.sync.dma_start(T.pack[:, C2 + 2:C2 + 4], T.x2[:, :]).then_inc(sem.loaded, 16)
+    g.wait_ge(sem.loaded, 64)
+
+    transfers = []
+    for k in range(NB):
+        owners = [c for c in (k, k + NB) if c != core]
+        transfers.append(RemoteDMATransfer(
+            dst_ids=[dst(c) for c in owners],
+            dma_engine_mask=0xF << (4 * k),
+            remote_sem=sem.arrived,
+            srcs=[blk(T.pack, k)],
+            dsts=[blk(T.land, core) for _c in owners],
+            alu_op=0))
+    g.remote_dma_fused(transfers, local_sem=sem.sent)
+
+    g.wait_ge(sem.arrived, 7 * 4)
+    die_base = core - mine
+    targets = [c for c in range(die_base, die_base + NB) if c != core] + [partner]
+    g.remote_dma_fused([RemoteDMATransfer(
+        dst_ids=[dst(c) for c in targets],
+        dma_engine_mask=0xFFFF,
+        remote_sem=sem.summed,
+        srcs=[blk(T.pack, mine)] + [blk(T.land, s) for s in range(8) if s != core],
+        dsts=[blk(T.res, mine) for _c in targets],
+        alu_op=1)], local_sem=sem.sent)
+
+    g.sync.wait_ge(sem.summed, 4 * 16)
+    g.sync.dma_start(T.y1[:, :], T.res[:, C1:C1 + 256]).then_inc(sem.stored, 16)
+    g.scalar.wait_ge(sem.summed, 4 * 16)
+    g.scalar.dma_start(T.y3[:, :], T.res[:, C3:C3 + 64]).then_inc(sem.stored, 16)
+    g.scalar.dma_start(T.y2[:, :], T.res[:, C2:C2 + 2]).then_inc(sem.stored, 16)
+
+    g.wait_ge(sem.sent, 32)
+    g.wait_ge(sem.summed, 4 * 16)
+    g.wait_ge(sem.stored, 48)

@@ -1,13 +1,16 @@
 from concourse.bass import DstId, RemoteDMATransfer
 
-W = 81
-NB = 4
-C1, C3, C2 = 0, 256, 320
+N = 32
+ROWS = 1288
+NPIECE = 11
+PIECES = [[0, 1, 8], [2, 3, 9], [4, 5, 10], [6, 7]]
+FOLD_ENGINES = {3: [8, 4, 4], 2: [8, 8]}
+MAXOWN = 3
 
 SCRATCH = {
-    "pack": ("sbuf", [128, NB * W], "float32"),
-    "land": ("sbuf", [128, 8 * W], "float32"),
-    "res": ("sbuf", [128, NB * W], "float32"),
+    "pack": ("dram", [ROWS, N], "float32"),
+    "land": ("dram", [8 * MAXOWN, 128, N], "float32"),
+    "res": ("dram", [NPIECE * 128, N], "float32"),
 }
 SEMAPHORES = ["loaded", "arrived", "summed", "sent", "stored"]
 
@@ -21,47 +24,58 @@ def rank_program(g, core, T, topo):
         rid, pid, _se = topo.addr(c)
         return DstId(rid=rid, pnc=pid)
 
-    def blk(buf, k):
-        return buf[:, k * W:(k + 1) * W]
+    def packed(t):
+        first = min(128 * t, ROWS - 128)
+        return T.pack[first:first + 128, :]
 
-    mine = core % NB
-    partner = (core + NB) % 8
+    def summed(t):
+        return T.res[128 * t:128 * t + 128, :]
 
-    g.sync.dma_start(T.pack[:, C1:C1 + 256], T.x1[:, :]).then_inc(sem.loaded, 16)
-    g.scalar.dma_start(T.pack[:, C3:C3 + 64], T.x3[:, :]).then_inc(sem.loaded, 16)
-    g.scalar.dma_start(T.pack[:, C2:C2 + 2], T.x2[:, :]).then_inc(sem.loaded, 16)
-    g.sync.dma_start(T.pack[:, C2 + 2:C2 + 4], T.x2[:, :]).then_inc(sem.loaded, 16)
-    g.wait_ge(sem.loaded, 64)
+    pair = core % 4
+    partner = (core + 4) % 8
+    own = PIECES[pair]
+
+    g.sync.dma_start(T.pack[0:1024, :], T.x1[:, :]).then_inc(sem.loaded, 16)
+    g.scalar.dma_start(T.pack[1024:1280, :], T.x3[:, :]).then_inc(sem.loaded, 16)
+    g.scalar.dma_start(T.pack[1280:1288, :], T.x2[:, :]).then_inc(sem.loaded, 16)
+    g.wait_ge(sem.loaded, 48)
 
     transfers = []
-    for k in range(NB):
-        owners = [c for c in (k, k + NB) if c != core]
-        transfers.append(RemoteDMATransfer(
-            dst_ids=[dst(c) for c in owners],
-            dma_engine_mask=0xF << (4 * k),
-            remote_sem=sem.arrived,
-            srcs=[blk(T.pack, k)],
-            dsts=[blk(T.land, core) for _c in owners],
-            alu_op=0))
+    for k in range(4):
+        owners = [c for c in (k, k + 4) if c != core]
+        for j, t in enumerate(PIECES[k]):
+            transfers.append(RemoteDMATransfer(
+                dst_ids=[dst(c) for c in owners],
+                dma_engine_mask=1 << t,
+                remote_sem=sem.arrived,
+                srcs=[packed(t)],
+                dsts=[T.land[MAXOWN * core + j] for _c in owners],
+                alu_op=0))
     g.remote_dma_fused(transfers, local_sem=sem.sent)
 
-    g.wait_ge(sem.arrived, 7 * 4)
-    die_base = core - mine
-    targets = [c for c in range(die_base, die_base + NB) if c != core] + [partner]
-    g.remote_dma_fused([RemoteDMATransfer(
-        dst_ids=[dst(c) for c in targets],
-        dma_engine_mask=0xFFFF,
-        remote_sem=sem.summed,
-        srcs=[blk(T.pack, mine)] + [blk(T.land, s) for s in range(8) if s != core],
-        dsts=[blk(T.res, mine) for _c in targets],
-        alu_op=1)], local_sem=sem.sent)
+    g.wait_ge(sem.arrived, 7 * len(own))
+    die_base = core - pair
+    targets = [c for c in range(die_base, die_base + 4) if c != core] + [partner]
+    transfers = []
+    first = 0
+    for j, t in enumerate(own):
+        n_eng = FOLD_ENGINES[len(own)][j]
+        transfers.append(RemoteDMATransfer(
+            dst_ids=[dst(c) for c in targets],
+            dma_engine_mask=((1 << n_eng) - 1) << first,
+            remote_sem=sem.summed,
+            srcs=[packed(t)] + [T.land[MAXOWN * s + j] for s in range(8) if s != core],
+            dsts=[summed(t) for _c in targets],
+            alu_op=1))
+        first += n_eng
+    g.remote_dma_fused(transfers, local_sem=sem.sent)
 
-    g.sync.wait_ge(sem.summed, 4 * 16)
-    g.sync.dma_start(T.y1[:, :], T.res[:, C1:C1 + 256]).then_inc(sem.stored, 16)
-    g.scalar.wait_ge(sem.summed, 4 * 16)
-    g.scalar.dma_start(T.y3[:, :], T.res[:, C3:C3 + 64]).then_inc(sem.stored, 16)
-    g.scalar.dma_start(T.y2[:, :], T.res[:, C2:C2 + 2]).then_inc(sem.stored, 16)
+    g.sync.wait_ge(sem.summed, 64)
+    g.sync.dma_start(T.y1[:, :], T.res[0:1024, :]).then_inc(sem.stored, 16)
+    g.scalar.wait_ge(sem.summed, 64)
+    g.scalar.dma_start(T.y3[:, :], T.res[1024:1280, :]).then_inc(sem.stored, 16)
+    g.scalar.dma_start(T.y2[:, :], T.res[1400:1408, :]).then_inc(sem.stored, 16)
 
-    g.wait_ge(sem.sent, 32)
-    g.wait_ge(sem.summed, 4 * 16)
+    g.wait_ge(sem.sent, NPIECE + 16)
+    g.wait_ge(sem.summed, 64)
     g.wait_ge(sem.stored, 48)

from concourse.bass import DstId, RemoteDMATransfer

N = 32
ROWS = 1288
NPIECE = 11
PIECES = [[0, 1, 8], [2, 3, 9], [4, 5, 10], [6, 7]]
FOLD_ENGINES = {3: [8, 4, 4], 2: [8, 8]}
MAXOWN = 3

SCRATCH = {
    "pack": ("dram", [ROWS, N], "float32"),
    "land": ("dram", [8 * MAXOWN, 128, N], "float32"),
    "res": ("dram", [NPIECE * 128, N], "float32"),
}
SEMAPHORES = ["loaded", "arrived", "summed", "sent", "stored"]


def rank_program(g, core, T, topo):
    if T.rank_of(core) is None:
        return
    sem = T.sem

    def dst(c):
        rid, pid, _se = topo.addr(c)
        return DstId(rid=rid, pnc=pid)

    def packed(t):
        first = min(128 * t, ROWS - 128)
        return T.pack[first:first + 128, :]

    def summed(t):
        return T.res[128 * t:128 * t + 128, :]

    pair = core % 4
    partner = (core + 4) % 8
    own = PIECES[pair]

    g.sync.dma_start(T.pack[0:1024, :], T.x1[:, :]).then_inc(sem.loaded, 16)
    g.scalar.dma_start(T.pack[1024:1280, :], T.x3[:, :]).then_inc(sem.loaded, 16)
    g.scalar.dma_start(T.pack[1280:1288, :], T.x2[:, :]).then_inc(sem.loaded, 16)
    g.wait_ge(sem.loaded, 48)

    transfers = []
    for k in range(4):
        owners = [c for c in (k, k + 4) if c != core]
        for j, t in enumerate(PIECES[k]):
            transfers.append(RemoteDMATransfer(
                dst_ids=[dst(c) for c in owners],
                dma_engine_mask=1 << t,
                remote_sem=sem.arrived,
                srcs=[packed(t)],
                dsts=[T.land[MAXOWN * core + j] for _c in owners],
                alu_op=0))
    g.remote_dma_fused(transfers, local_sem=sem.sent)

    g.wait_ge(sem.arrived, 7 * len(own))
    die_base = core - pair
    targets = [c for c in range(die_base, die_base + 4) if c != core] + [partner]
    transfers = []
    first = 0
    for j, t in enumerate(own):
        n_eng = FOLD_ENGINES[len(own)][j]
        transfers.append(RemoteDMATransfer(
            dst_ids=[dst(c) for c in targets],
            dma_engine_mask=((1 << n_eng) - 1) << first,
            remote_sem=sem.summed,
            srcs=[packed(t)] + [T.land[MAXOWN * s + j] for s in range(8) if s != core],
            dsts=[summed(t) for _c in targets],
            alu_op=1))
        first += n_eng
    g.remote_dma_fused(transfers, local_sem=sem.sent)

    g.sync.wait_ge(sem.summed, 64)
    g.sync.dma_start(T.y1[:, :], T.res[0:1024, :]).then_inc(sem.stored, 16)
    g.scalar.wait_ge(sem.summed, 64)
    g.scalar.dma_start(T.y3[:, :], T.res[1024:1280, :]).then_inc(sem.stored, 16)
    g.scalar.dma_start(T.y2[:, :], T.res[1400:1408, :]).then_inc(sem.stored, 16)

    g.wait_ge(sem.sent, NPIECE + 16)
    g.wait_ge(sem.summed, 64)
    g.wait_ge(sem.stored, 48)
